import numpy as np
import ml_dtypes

BF16 = ml_dtypes.bfloat16


def bf(x):
    return np.asarray(x, np.float32).astype(BF16)


def f32(x):
    return np.asarray(x, np.float32)


def f64(x):
    return np.asarray(x).astype(np.float64)


def striped(idx):
    return np.tile(idx.reshape(-1, 16).T, (8, 1))


S, K, M, N, B, Q = 256, 128, 256, 256, 2, 128


def gelu_tanh(v):
    return 0.5 * v * (1.0 + np.tanh(np.sqrt(2.0 / np.pi) * (v + 0.044715 * v**3)))


def setup_inputs():
    return {"base": bf(np.random.standard_normal((B, M, S))), "x": bf(np.random.standard_normal((K, N))), "w": bf(np.random.standard_normal((K, M)) / np.sqrt(K)), "b": f32(0.5 * np.random.standard_normal((M, 1))), "offs": striped(np.random.permutation(S))}


def reference(base, x, w, b, offs):
    idx = offs[:16].T.reshape(-1)
    z = f64(base).copy()
    for i in range(B):
        z[i][:, idx[i * Q : (i + 1) * Q]] += f64(w).T @ f64(x)[:, i * Q : (i + 1) * Q]
    return gelu_tanh(z + f64(b))

@@ -1,0 +1,55 @@
+import concourse.mybir as mybir
+from concourse.masks import make_identity
+
+BF16, F32, U16 = mybir.dt.bfloat16, mybir.dt.float32, mybir.dt.uint16
+GELU_TANH = mybir.ActivationFunctionType.Gelu_apprx_tanh
+
+P = 128
+B, M, S = 2, 256, 256
+K, N = 128, 256
+Q = N // B
+A = M // P
+FLOPS = 2 * K * M * N
+
+
+def tile_scatter_matmul_kernel(tc, base, x, w, b, offs, out):
+    nc = tc.nc
+    with (
+        tc.tile_pool(name="held", bufs=1) as held,
+        tc.psum_pool(name="psum", bufs=1) as psum,
+    ):
+        base_t = held.tile([P, B, A, S], BF16, name="base_t")
+        for i in range(B):
+            nc.sync.dma_start(base_t[:, i], base[i].rearrange("(a p) t -> p a t", p=P))
+        w_t = held.tile([K, M], BF16, name="w_t")
+        nc.sync.dma_start(w_t[:], w)
+        x_t = held.tile([K, N], BF16, name="x_t")
+        nc.sync.dma_start(x_t[:], x)
+        offsets = held.tile([P, N // 16], U16, name="offsets")
+        nc.sync.dma_start(offsets[:], offs)
+        bias = held.tile([P, A], F32, name="bias")
+        nc.sync.dma_start(bias[:], b.rearrange("(a p) o -> p (a o)", p=P))
+
+        ident = held.tile([P, P], BF16, name="ident")
+        make_identity(nc, ident[:])
+
+        blocks = [(i, a) for i in range(B) for a in range(A)]
+        windows = {(i, a): psum.tile([P, S], F32, name=f"window{i}{a}") for i, a in blocks}
+
+        for i, a in blocks:
+            nc.tensor.matmul(windows[i, a][:], ident[:], base_t[:, i, a], start=True, stop=False)
+
+        for i, a in blocks:
+            places = offsets[:, i * Q // 16 : (i + 1) * Q // 16]
+            nc.tensor.matmul(
+                windows[i, a][:].indirect(places),
+                w_t[:, a * P : (a + 1) * P],
+                x_t[:, i * Q : (i + 1) * Q],
+                start=False,
+                stop=True,
+            )
+
+        for i, a in blocks:
+            result = held.tile([P, S], F32, name=f"result{i}{a}")
+            nc.scalar.activation(result[:], windows[i, a][:], GELU_TANH, bias=bias[:, a : a + 1])
+            nc.sync.dma_start(out[i, a * P : (a + 1) * P], result[:])

@@ -18,6 +18,11 @@ def tile_scatter_matmul_kernel(tc, base, x, w, b, offs, out):
         tc.tile_pool(name="held", bufs=1) as held,
         tc.psum_pool(name="psum", bufs=1) as psum,
     ):
+        zero = held.tile([P, 1], F32, name="zero")
+        nc.vector.memset(zero[:], 0.0)
+        early = held.tile([P, 1], F32, name="early")
+        nc.scalar.activation(early[:], zero[:], GELU_TANH, bias=zero[:])
+
         base_t = held.tile([P, B, A, S], BF16, name="base_t")
         for i in range(B):
             nc.sync.dma_start(base_t[:, i], base[i].rearrange("(a p) t -> p a t", p=P))

@@ -9,6 +9,7 @@ B, M, S = 2, 256, 256
 K, N = 128, 256
 Q = N // B
 A = M // P
+WARM_UPS = 12
 FLOPS = 2 * K * M * N
 
 
@@ -18,6 +19,12 @@ def tile_scatter_matmul_kernel(tc, base, x, w, b, offs, out):
         tc.tile_pool(name="held", bufs=1) as held,
         tc.psum_pool(name="psum", bufs=1) as psum,
     ):
+        blank = held.tile([P, P], BF16, name="blank")
+        nc.vector.memset(blank[:], 0.0)
+        spare = psum.tile([P, P], F32, name="spare")
+        for warm in range(WARM_UPS):
+            nc.tensor.matmul(spare[:], blank[:], blank[:], start=True, stop=True)
+
         zero = held.tile([P, 1], F32, name="zero")
         nc.vector.memset(zero[:], 0.0)
         early = held.tile([P, 1], F32, name="early")
@@ -25,7 +32,7 @@ def tile_scatter_matmul_kernel(tc, base, x, w, b, offs, out):
 
         base_t = held.tile([P, B, A, S], BF16, name="base_t")
         for i in range(B):
-            nc.sync.dma_start(base_t[:, i], base[i].rearrange("(a p) t -> p a t", p=P))
+            nc.sync.dma_start(base_t[:, i], base[i].rearrange("(p a) t -> p a t", a=A))
         w_t = held.tile([K, M], BF16, name="w_t")
         nc.sync.dma_start(w_t[:], w)
         x_t = held.tile([K, N], BF16, name="x_t")
@@ -33,7 +40,7 @@ def tile_scatter_matmul_kernel(tc, base, x, w, b, offs, out):
         offsets = held.tile([P, N // 16], U16, name="offsets")
         nc.sync.dma_start(offsets[:], offs)
         bias = held.tile([P, A], F32, name="bias")
-        nc.sync.dma_start(bias[:], b.rearrange("(a p) o -> p (a o)", p=P))
+        nc.sync.dma_start(bias[:], b.rearrange("(p a) o -> p (a o)", a=A))
 
         ident = held.tile([P, P], BF16, name="ident")
         make_identity(nc, ident[:])
@@ -48,7 +55,7 @@ def tile_scatter_matmul_kernel(tc, base, x, w, b, offs, out):
             places = offsets[:, i * Q // 16 : (i + 1) * Q // 16]
             nc.tensor.matmul(
                 windows[i, a][:].indirect(places),
-                w_t[:, a * P : (a + 1) * P],
+                w_t[:, a::A],
                 x_t[:, i * Q : (i + 1) * Q],
                 start=False,
                 stop=True,
@@ -57,4 +64,4 @@ def tile_scatter_matmul_kernel(tc, base, x, w, b, offs, out):
         for i, a in blocks:
             result = held.tile([P, S], F32, name=f"result{i}{a}")
             nc.scalar.activation(result[:], windows[i, a][:], GELU_TANH, bias=bias[:, a : a + 1])
-            nc.sync.dma_start(out[i, a * P : (a + 1) * P], result[:])
+            nc.sync.dma_start(out[i].rearrange("(p a) t -> p a t", a=A)[:, a], result[:])

import concourse.mybir as mybir
from concourse.masks import make_identity

BF16, F32, U16 = mybir.dt.bfloat16, mybir.dt.float32, mybir.dt.uint16
GELU_TANH = mybir.ActivationFunctionType.Gelu_apprx_tanh

P = 128
B, M, S = 2, 256, 256
K, N = 128, 256
Q = N // B
A = M // P
WARM_UPS = 12
FLOPS = 2 * K * M * N


def tile_scatter_matmul_kernel(tc, base, x, w, b, offs, out):
    nc = tc.nc
    with (
        tc.tile_pool(name="held", bufs=1) as held,
        tc.psum_pool(name="psum", bufs=1) as psum,
    ):
        blank = held.tile([P, P], BF16, name="blank")
        nc.vector.memset(blank[:], 0.0)
        spare = psum.tile([P, P], F32, name="spare")
        for warm in range(WARM_UPS):
            nc.tensor.matmul(spare[:], blank[:], blank[:], start=True, stop=True)

        zero = held.tile([P, 1], F32, name="zero")
        nc.vector.memset(zero[:], 0.0)
        early = held.tile([P, 1], F32, name="early")
        nc.scalar.activation(early[:], zero[:], GELU_TANH, bias=zero[:])

        base_t = held.tile([P, B, A, S], BF16, name="base_t")
        for i in range(B):
            nc.sync.dma_start(base_t[:, i], base[i].rearrange("(p a) t -> p a t", a=A))
        w_t = held.tile([K, M], BF16, name="w_t")
        nc.sync.dma_start(w_t[:], w)
        x_t = held.tile([K, N], BF16, name="x_t")
        nc.sync.dma_start(x_t[:], x)
        offsets = held.tile([P, N // 16], U16, name="offsets")
        nc.sync.dma_start(offsets[:], offs)
        bias = held.tile([P, A], F32, name="bias")
        nc.sync.dma_start(bias[:], b.rearrange("(p a) o -> p (a o)", a=A))

        ident = held.tile([P, P], BF16, name="ident")
        make_identity(nc, ident[:])

        blocks = [(i, a) for i in range(B) for a in range(A)]
        windows = {(i, a): psum.tile([P, S], F32, name=f"window{i}{a}") for i, a in blocks}

        for i, a in blocks:
            nc.tensor.matmul(windows[i, a][:], ident[:], base_t[:, i, a], start=True, stop=False)

        for i, a in blocks:
            places = offsets[:, i * Q // 16 : (i + 1) * Q // 16]
            nc.tensor.matmul(
                windows[i, a][:].indirect(places),
                w_t[:, a::A],
                x_t[:, i * Q : (i + 1) * Q],
                start=False,
                stop=True,
            )

        for i, a in blocks:
            result = held.tile([P, S], F32, name=f"result{i}{a}")
            nc.scalar.activation(result[:], windows[i, a][:], GELU_TANH, bias=bias[:, a : a + 1])
            nc.sync.dma_start(out[i].rearrange("(p a) t -> p a t", a=A)[:, a], result[:])
